import numpy as np, ml_dtypes
CORES = [0,1,2,3]
N = 4
def setup_inputs(rng):
    return {"x": rng.standard_normal((N, 128, 512), dtype=np.float32).astype(ml_dtypes.bfloat16)}
def reference(x):
    s = x.sum(axis=0, dtype=np.float64).astype(x.dtype)
    p = 128 // N
    return {"y": np.stack([s[r * p:(r + 1) * p, :] for r in range(N)])}

@@ -1,0 +1,57 @@
+from concourse.bass import DstId, RemoteDMATransfer
+from concourse.mybir import AluOpType
+
+N = 4
+PIECE = 128
+
+SCRATCH = {
+    "stage": ("dram", [N, 128, PIECE], "bfloat16"),
+    "land": ("dram", [2, 128, PIECE], "bfloat16"),
+    "res": ("dram", [128, PIECE], "bfloat16"),
+}
+SEMAPHORES = ["staged", "preset", "stored", "sent", "parts", "total"]
+
+LOW, HIGH, ALL = 0x00FF, 0xFF00, 0xFFFF
+
+
+def rank_program(g, core, T, topo):
+    r = T.rank_of(core)
+    if r is None:
+        return
+
+    rows = T.y.shape[0]
+    nxt, opp, prv = (r + 1) % N, (r + 2) % N, (r + 3) % N
+
+    def dst(rank):
+        rid, pid, _se = topo.addr(T.cores[rank])
+        return DstId(rid=rid, pnc=pid)
+
+    g.dma_start(T.stage[:], T.x[:]).then_inc(T.sem.staged, 16)
+    g.dma_start(T.y[:], T.x[r * rows:(r + 1) * rows, :]).then_inc(T.sem.preset, 16)
+
+    g.wait_ge(T.sem.staged, 16)
+    g.remote_dma_fused(
+        [
+            RemoteDMATransfer(dst_ids=[dst(nxt)], dma_engine_mask=LOW, remote_sem=T.sem.parts,
+                              src=T.stage[prv], dst=T.land[0]),
+            RemoteDMATransfer(dst_ids=[dst(prv)], dma_engine_mask=HIGH, remote_sem=T.sem.parts,
+                              src=T.stage[nxt], dst=T.land[1]),
+        ],
+        local_sem=T.sem.sent,
+    )
+
+    g.wait_ge(T.sem.parts, 16)
+    g.remote_dma_fused(
+        [
+            RemoteDMATransfer(dst_ids=[dst(opp)], dma_engine_mask=ALL, remote_sem=T.sem.total,
+                              srcs=[T.stage[opp], T.land[0], T.land[1]], dsts=[T.res[:]], alu_op=1),
+        ],
+        local_sem=T.sem.sent,
+    )
+
+    g.wait_ge(T.sem.preset, 16)
+    g.wait_ge(T.sem.total, 16)
+    g.dma_start(T.y[:], T.res[:], accum_op=AluOpType.add, max_dma_last_dim=4096).then_inc(T.sem.stored, 16)
+    g.wait_ge(T.sem.stored, 16)
+
+    g.wait_ge(T.sem.sent, 32)

@@ -23,7 +23,7 @@ def rank_program(g, core, T, topo):
     nxt, opp, prv = (r + 1) % N, (r + 2) % N, (r + 3) % N
 
     def dst(rank):
-        rid, pid, _se = topo.addr(T.cores[rank])
+        rid, pid = topo.addr(T.cores[rank])[:2]
         return DstId(rid=rid, pnc=pid)
 
     g.dma_start(T.stage[:], T.x[:]).then_inc(T.sem.staged, 16)

from concourse.bass import DstId, RemoteDMATransfer
from concourse.mybir import AluOpType

N = 4
PIECE = 128

SCRATCH = {
    "stage": ("dram", [N, 128, PIECE], "bfloat16"),
    "land": ("dram", [2, 128, PIECE], "bfloat16"),
    "res": ("dram", [128, PIECE], "bfloat16"),
}
SEMAPHORES = ["staged", "preset", "stored", "sent", "parts", "total"]

LOW, HIGH, ALL = 0x00FF, 0xFF00, 0xFFFF


def rank_program(g, core, T, topo):
    r = T.rank_of(core)
    if r is None:
        return

    rows = T.y.shape[0]
    nxt, opp, prv = (r + 1) % N, (r + 2) % N, (r + 3) % N

    def dst(rank):
        rid, pid = topo.addr(T.cores[rank])[:2]
        return DstId(rid=rid, pnc=pid)

    g.dma_start(T.stage[:], T.x[:]).then_inc(T.sem.staged, 16)
    g.dma_start(T.y[:], T.x[r * rows:(r + 1) * rows, :]).then_inc(T.sem.preset, 16)

    g.wait_ge(T.sem.staged, 16)
    g.remote_dma_fused(
        [
            RemoteDMATransfer(dst_ids=[dst(nxt)], dma_engine_mask=LOW, remote_sem=T.sem.parts,
                              src=T.stage[prv], dst=T.land[0]),
            RemoteDMATransfer(dst_ids=[dst(prv)], dma_engine_mask=HIGH, remote_sem=T.sem.parts,
                              src=T.stage[nxt], dst=T.land[1]),
        ],
        local_sem=T.sem.sent,
    )

    g.wait_ge(T.sem.parts, 16)
    g.remote_dma_fused(
        [
            RemoteDMATransfer(dst_ids=[dst(opp)], dma_engine_mask=ALL, remote_sem=T.sem.total,
                              srcs=[T.stage[opp], T.land[0], T.land[1]], dsts=[T.res[:]], alu_op=1),
        ],
        local_sem=T.sem.sent,
    )

    g.wait_ge(T.sem.preset, 16)
    g.wait_ge(T.sem.total, 16)
    g.dma_start(T.y[:], T.res[:], accum_op=AluOpType.add, max_dma_last_dim=4096).then_inc(T.sem.stored, 16)
    g.wait_ge(T.sem.stored, 16)

    g.wait_ge(T.sem.sent, 32)
